import numpy as np
import ml_dtypes


def mxq(x, axis, fmt="e4m3"):
    dtype, down = {"e4m3": (ml_dtypes.float8_e4m3fn, 7), "e5m2": (ml_dtypes.float8_e5m2, 14)}[fmt]
    v = np.moveaxis(np.asarray(x, np.float32).astype(ml_dtypes.bfloat16).astype(np.float64), axis, -1)
    blocks = v.reshape(v.shape[:-1] + (-1, 32))
    amax = np.abs(blocks).max(-1, keepdims=True)
    byte = np.maximum(np.where(amax > 0, np.frexp(amax)[1] - 1 + 127, 0) - down, 1)
    scale = np.exp2(byte - 127.0)
    codes = (blocks / scale).astype(np.float32).astype(dtype).astype(np.float64)
    return np.moveaxis((codes * scale).reshape(v.shape), -1, axis)


WIDE = False


def mx_kscale(k):
    if not WIDE:
        return np.ones(k)
    levels = np.array([10, -10, 5, -5, 0])
    if k % 512:
        return np.exp2(np.random.permutation(np.resize(levels, k // 32))).repeat(32)
    a = np.empty((k // 512, 16))
    for p in range(k // 512):
        a[p, :8] = np.random.permutation(np.resize(levels, 8))
        for g in range(8):
            far = levels[np.abs(levels - a[p, g]) >= 10]
            a[p, g + 8] = far[np.random.randint(len(far))]
    return np.exp2(a.ravel()).repeat(32)


def f64(x):
    return np.asarray(x).astype(np.float64)


def striped(idx):
    return np.tile(idx.reshape(-1, 16).T, (8, 1)).astype(np.uint16)


def unstriped(offs):
    return offs[:16].T.reshape(-1).astype(np.int64)


E2M1 = np.array([0.0, 0.5, 1.0, 1.5, 2.0, 3.0, 4.0, 6.0, -0.0, -0.5, -1.0, -1.5, -2.0, -3.0, -4.0, -6.0])


def pack_weight(w, fmt):
    k, n = w.shape
    w = f64(np.asarray(w, np.float32).astype(ml_dtypes.bfloat16)).reshape(k // 32, 32, n)
    amax = np.abs(w).max(1)
    if fmt == "e4m3":
        byte = np.frexp(amax)[1] - 1 + 127 - 7
    else:
        mant, ex = np.frexp(amax / 6.0)
        byte = np.where(mant > 0.5, ex, ex - 1) + 127
    byte = np.clip(np.where(amax > 0, byte, 1), 1, 254)
    scaled = (w * np.exp2(127.0 - byte)[:, None, :]).reshape(k, n).astype(np.float32)
    by_word = np.ascontiguousarray(scaled.reshape(k // 512, 128, 4, n).transpose(0, 1, 3, 2))
    if fmt == "e4m3":
        words = by_word.astype(ml_dtypes.float8_e4m3fn).view(np.uint8)
    else:
        c = by_word.astype(ml_dtypes.float4_e2m1fn).view(np.uint8) & 0xF
        words = (c[..., 0::2] | (c[..., 1::2] << 4)).reshape(k // 512, 128, 2 * n)
    return np.ascontiguousarray(words), np.ascontiguousarray(byte.astype(np.uint8).reshape(k // 512, 16, n))


def unpack_weight(words, scales, fmt):
    g, _, n = scales.shape
    words = np.ascontiguousarray(words).reshape(g, 128, n, -1)
    if fmt == "e4m3":
        vals = words.view(ml_dtypes.float8_e4m3fn).astype(np.float64)
    else:
        nib = np.empty((g, 128, n, 4), np.uint8)
        nib[..., 0::2] = words & 0xF
        nib[..., 1::2] = words >> 4
        vals = E2M1[nib]
    vals = vals * np.repeat(np.exp2(scales.astype(np.float64) - 127.0), 8, axis=1)[..., None]
    return vals.transpose(0, 1, 3, 2).reshape(g * 512, n)


def gelu(v):
    return 0.5 * v * (1.0 + np.tanh(np.sqrt(2.0 / np.pi) * (v + 0.044715 * v**3)))


K, T, E1, C1, E2, C2, H = 512, 512, 4, 128, 2, 256, 512
N = 256


def by_expert(wq, xq, E, C):
    return np.concatenate([wq[e].T @ xq[:, e * C:(e + 1) * C] for e in range(E)], axis=1)


def setup_inputs():
    n = np.random.standard_normal
    s = mx_kscale(K)
    u = mx_kscale(H)
    slots1, slots2 = np.random.permutation(T), np.random.permutation(T)
    x = pack_weight(n((K, T)) * s[:, None], "e4m3")
    wa = [pack_weight(m, "e2m1") for m in n((E1, K, H)) / np.sqrt(K) / s[None, :, None]]
    wb = [pack_weight(m, "e2m1") for m in n((E2, K, H)) / np.sqrt(K) / s[None, :, None] * u]
    w2 = pack_weight(n((H, N)) / np.sqrt(H) / u[:, None], "e2m1")
    return {
        "x_words": x[0],
        "x_scales": x[1],
        "wa_words": np.stack([m[0] for m in wa]),
        "wa_scales": np.stack([m[1] for m in wa]),
        "wb_words": np.stack([m[0] for m in wb]),
        "wb_scales": np.stack([m[1] for m in wb]),
        "w2_words": w2[0],
        "w2_scales": w2[1],
        "offs": striped(slots1),
        "offs2": striped(slots2),
    }


def reference(x_words, x_scales, wa_words, wa_scales, wb_words, wb_scales, w2_words, w2_scales, offs, offs2):
    wa = np.stack([unpack_weight(wa_words[e], wa_scales[e], "e2m1") for e in range(E1)])
    wb = np.stack([unpack_weight(wb_words[e], wb_scales[e], "e2m1") for e in range(E2)])
    w2 = unpack_weight(w2_words, w2_scales, "e2m1")
    idx, idx2 = unstriped(offs), unstriped(offs2)
    x = unpack_weight(x_words, x_scales, "e4m3")
    a, c = np.zeros((H, T)), np.zeros((H, T))
    a[:, idx] = by_expert(wa, x[:, idx], E1, C1)
    c[:, idx2] = by_expert(wb, x[:, idx2], E2, C2)
    return w2.T @ mxq(gelu(a) * c, 0, "e4m3")

@@ -1,0 +1,162 @@
+from contextlib import ExitStack
+
+import concourse.mybir as mybir
+from concourse.masks import make_identity
+
+K, T, H, N = 512, 512, 512, 256
+E1, E2 = 4, 2
+FLOPS = 2 * K * H * T * 2 + 2 * H * N * T
+
+F32 = mybir.dt.float32
+BF16 = mybir.dt.bfloat16
+I32 = mybir.dt.int32
+U32 = mybir.dt.uint32
+U16 = mybir.dt.uint16
+U8 = mybir.dt.uint8
+FP8X4 = mybir.dt.float8_e4m3fn_x4
+FP4X4 = mybir.dt.float4_e2m1fn_x4
+GELU = mybir.ActivationFunctionType.Gelu_apprx_tanh
+MULT = mybir.AluOpType.mult
+
+P = 128
+PACK = 4
+BLOCK = 128
+WIDE = 704
+HALF = T // 2
+
+
+def tile_moe_pool_gelu_kernel(
+    tc, x_words, x_scales, wa_words, wa_scales, wb_words, wb_scales, w2_words, w2_scales, offs, offs2, out
+):
+    nc = tc.nc
+    with ExitStack() as ctx:
+        keep = ctx.enter_context(tc.tile_pool(name="keep", bufs=1))
+        stage = ctx.enter_context(tc.tile_pool(name="stage", bufs=3))
+        psum = ctx.enter_context(tc.psum_pool(name="psum", bufs=8))
+
+        def held(name, shape, dtype):
+            return keep.tile(shape, dtype, name=name, align_bytes=64)
+
+        list_a = held("list_a", [P, T // 16], U16)
+        list_c = held("list_c", [P, T // 16], U16)
+        xw = held("xw", [P, T], I32)
+        xs = held("xs", [P, T], U8)
+        wa = [held("wa%d" % g, [P, 2, 2 * H], U8) for g in range(2)]
+        wb = [held("wb%d" % f, [P, 2 * H], U8) for f in range(E2)]
+        was = held("was", [P, E1, H], U8)
+        wbs = held("wbs", [P, E2, H], U8)
+        w2 = held("w2", [P, 2 * N], U8)
+        w2s = held("w2s", [P, N], U8)
+        ident = held("ident", [P, P], F32)
+        warm = held("warm", [P, 8], F32)
+
+        nc.vector.memset(xs[:].bitcast(I32), 0)
+        nc.vector.memset(wbs[:].bitcast(I32), 0)
+        nc.vector.memset(was[:].bitcast(I32), 0)
+        nc.vector.memset(w2s[:].bitcast(I32), 0)
+
+        def load_scales(plane, rows):
+            for q in range(4):
+                nc.sync.dma_start(plane[32 * q : 32 * q + 4].bitcast(I32), rows(q).bitcast(I32))
+
+        nc.sync.dma_start(list_c[:], offs2)
+        nc.scalar.dma_start(xw[:], x_words[0].rearrange("p t d -> p (t d)").bitcast(I32))
+        load_scales(xs, lambda q: x_scales[0, 4 * q : 4 * q + 4, :])
+        nc.scalar.dma_start(wb[0][:].bitcast(I32), wb_words[0, 0].bitcast(I32))
+        load_scales(wbs, lambda q: wb_scales[:, 0, 4 * q : 4 * q + 4, :].rearrange("e b i -> b e i"))
+        nc.sync.dma_start(list_a[:], offs)
+        nc.sync.dma_start(wb[1][:].bitcast(I32), wb_words[1, 0].bitcast(I32))
+        for g in range(2):
+            nc.sync.dma_start(wa[g][:].bitcast(I32), wa_words[2 * g : 2 * g + 2, 0].rearrange("e p b -> p e b").bitcast(I32))
+        load_scales(was, lambda q: wa_scales[:, 0, 4 * q : 4 * q + 4, :].rearrange("e b i -> b e i"))
+        nc.sync.dma_start(w2[:].bitcast(I32), w2_words[0].bitcast(I32))
+        load_scales(w2s, lambda q: w2_scales[0, 4 * q : 4 * q + 4, :])
+
+        make_identity(nc, ident[:])
+        nc.scalar.activation(warm[:, 0:1], ident[:, 0:1], GELU)
+
+        def offsets(lst, lo, hi):
+            return lst[:, lo // 16 : hi // 16]
+
+        def gather(name, lst, lo, hi):
+            words = held(name + "w", [P, hi - lo], U32)
+            scales = held(name + "s", [P, hi - lo], U8)
+            nc.vector.tensor_copy(words[:], xw[:].bitcast(U32).indirect(offsets(lst, lo, hi)))
+            nc.vector.tensor_copy(scales[:], xs[:].indirect(offsets(lst, lo, hi)))
+            return [
+                (words[:, j : j + BLOCK], scales[:, j : j + BLOCK]) for j in range(0, hi - lo, BLOCK)
+            ]
+
+        tokens_c = gather("gc0", list_c, 0, BLOCK) + gather("gc1", list_c, BLOCK, T)
+        tokens_a = gather("ga0", list_a, 0, HALF) + gather("ga1", list_a, HALF, T)
+
+        def expert(tokens, w_words, w_scales, gated, dst):
+            sums = psum.tile([P, H], F32, name="bank")
+            nc.tensor.matmul_mx(
+                out=sums[:], lhsT=tokens[0].bitcast(FP8X4), lhsT_scale=tokens[1],
+                rhs=w_words.bitcast(FP4X4), rhs_scale=w_scales, start=True, stop=True,
+            )
+            rows = stage.tile([P, PACK, P], F32, name="rows")
+            by_t = sums[:].rearrange("s (p t) -> s t p", t=PACK)
+            if gated:
+                nc.scalar.activation(rows[:], by_t, GELU)
+            else:
+                nc.scalar.copy(rows[:], by_t)
+            turned = psum.tile([P, PACK, BLOCK], F32, name="bank")
+            for t in range(PACK):
+                nc.tensor.transpose(turned[:, t, :], rows[:, t, :], ident[:])
+            nc.scalar.copy(dst, turned[:])
+
+        c_first = held("c_first", [P, PACK, BLOCK], F32)
+        c_rest = held("c_rest", [P, PACK, T - BLOCK], F32)
+        g_slots = held("g_slots", [P, PACK, T], F32)
+        expert(tokens_c[0], wb[0][:], wbs[:, 0, :], False, c_first[:])
+        for s in range(1, 4):
+            expert(tokens_c[s], wb[s // 2][:], wbs[:, s // 2, :], False, c_rest[:, :, (s - 1) * BLOCK : s * BLOCK])
+        for e in range(E1):
+            expert(tokens_a[e], wa[e // 2][:, e % 2, :], was[:, e, :], True, g_slots[:, :, e * BLOCK : (e + 1) * BLOCK])
+
+        c_tok = [held("c_tok%d" % t, [P, T], F32) for t in range(PACK)]
+        g_tok = [held("g_tok%d" % t, [P, WIDE], F32) for t in range(PACK)]
+        for t in range(PACK):
+            nc.vector.tensor_copy(c_tok[t][:].indirect(offsets(list_c, 0, BLOCK)), c_first[:, t, :])
+        for t in range(PACK):
+            nc.vector.tensor_copy(c_tok[t][:].indirect(offsets(list_c, BLOCK, T)), c_rest[:, t, :])
+
+        h_pair = [held("h_pair%d" % u, [P, 2, T], BF16) for u in range(2)]
+        h = held("h", [P, T, PACK], BF16)
+
+        def product(t, lo, hi):
+            nc.vector.tensor_tensor(h_pair[t // 2][:, t % 2, lo:hi], g_tok[t][:, lo:hi], c_tok[t][:, lo:hi], MULT)
+
+        for t in range(PACK):
+            nc.vector.tensor_copy(g_tok[t][:].indirect(list_a[:]), g_slots[:, t, :])
+            if t > 0:
+                product(t - 1, 0, T)
+            if t == 2:
+                nc.scalar.copy(h[:, :, 0:2], h_pair[0][:].rearrange("p u x -> p x u"))
+        halves = [slice(0, HALF), slice(HALF, T)]
+        for cols in halves:
+            product(PACK - 1, cols.start, cols.stop)
+        for cols in halves:
+            nc.vector.tensor_copy(h[:, cols, 2:4], h_pair[1][:, :, cols].rearrange("p u x -> p x u"))
+        codes = [held("codes%d" % u, [P, HALF], U32) for u in range(2)]
+        planes = [held("planes%d" % u, [P, HALF], U8) for u in range(2)]
+        for u, cols in enumerate(halves):
+            nc.vector.quantize_mx(
+                out=codes[u][:].bitcast(FP8X4), scales=planes[u][:], in_=h[:, cols, :].rearrange("p x t -> p (x t)")
+            )
+        for u, cols in enumerate(halves):
+            for nb in range(N // P):
+                sums = psum.tile([P, HALF], F32, name="bank")
+                nc.tensor.matmul_mx(
+                    out=sums[:], lhsT=w2[:, 2 * P * nb : 2 * P * (nb + 1)].bitcast(FP4X4), lhsT_scale=w2s[:, P * nb : P * (nb + 1)],
+                    rhs=codes[u][:].bitcast(FP8X4), rhs_scale=planes[u][:], start=True, stop=True,
+                )
+                result = held("result%d%d" % (u, nb), [P, HALF], F32)
+                if nb == 0:
+                    nc.scalar.copy(result[:], sums[:])
+                    nc.scalar.dma_start(out[P * nb : P * (nb + 1), cols], result[:])
+                else:
+                    nc.vector.tensor_copy(result[:], sums[:])
+                    nc.sync.dma_start(out[P * nb : P * (nb + 1), cols], result[:])

@@ -31,8 +31,9 @@ def tile_moe_pool_gelu_kernel(
     nc = tc.nc
     with ExitStack() as ctx:
         keep = ctx.enter_context(tc.tile_pool(name="keep", bufs=1))
-        stage = ctx.enter_context(tc.tile_pool(name="stage", bufs=3))
-        psum = ctx.enter_context(tc.psum_pool(name="psum", bufs=8))
+        stage = ctx.enter_context(tc.tile_pool(name="stage", bufs=2))
+        psum = ctx.enter_context(tc.psum_pool(name="psum", bufs=2))
+        psum_out = ctx.enter_context(tc.psum_pool(name="psum_out", bufs=4))
 
         def held(name, shape, dtype):
             return keep.tile(shape, dtype, name=name, align_bytes=64)
@@ -41,45 +42,45 @@ def tile_moe_pool_gelu_kernel(
         list_c = held("list_c", [P, T // 16], U16)
         xw = held("xw", [P, T], I32)
         xs = held("xs", [P, T], U8)
-        wa = [held("wa%d" % g, [P, 2, 2 * H], U8) for g in range(2)]
         wb = [held("wb%d" % f, [P, 2 * H], U8) for f in range(E2)]
+        wa = held("wa", [P, E1, 2 * H], U8)
+        w2 = held("w2", [P, 2 * N], U8)
         was = held("was", [P, E1, H], U8)
         wbs = held("wbs", [P, E2, H], U8)
-        w2 = held("w2", [P, 2 * N], U8)
         w2s = held("w2s", [P, N], U8)
         ident = held("ident", [P, P], F32)
-        warm = held("warm", [P, 8], F32)
 
-        nc.vector.memset(xs[:].bitcast(I32), 0)
-        nc.vector.memset(wbs[:].bitcast(I32), 0)
+        nc.gpsimd.memset(xs[:].bitcast(I32), 0)
+        nc.gpsimd.memset(wbs[:].bitcast(I32), 0)
         nc.vector.memset(was[:].bitcast(I32), 0)
         nc.vector.memset(w2s[:].bitcast(I32), 0)
 
-        def load_scales(plane, rows):
+        def load_scales(queue, plane, rows):
             for q in range(4):
-                nc.sync.dma_start(plane[32 * q : 32 * q + 4].bitcast(I32), rows(q).bitcast(I32))
+                queue.dma_start(plane[32 * q : 32 * q + 4].bitcast(I32), rows(q).bitcast(I32))
 
-        nc.sync.dma_start(list_c[:], offs2)
         nc.scalar.dma_start(xw[:], x_words[0].rearrange("p t d -> p (t d)").bitcast(I32))
-        load_scales(xs, lambda q: x_scales[0, 4 * q : 4 * q + 4, :])
+        nc.sync.dma_start(list_c[:], offs2)
+        load_scales(nc.sync, xs, lambda q: x_scales[0, 4 * q : 4 * q + 4, :])
         nc.scalar.dma_start(wb[0][:].bitcast(I32), wb_words[0, 0].bitcast(I32))
-        load_scales(wbs, lambda q: wb_scales[:, 0, 4 * q : 4 * q + 4, :].rearrange("e b i -> b e i"))
         nc.sync.dma_start(list_a[:], offs)
-        nc.sync.dma_start(wb[1][:].bitcast(I32), wb_words[1, 0].bitcast(I32))
-        for g in range(2):
-            nc.sync.dma_start(wa[g][:].bitcast(I32), wa_words[2 * g : 2 * g + 2, 0].rearrange("e p b -> p e b").bitcast(I32))
-        load_scales(was, lambda q: wa_scales[:, 0, 4 * q : 4 * q + 4, :].rearrange("e b i -> b e i"))
-        nc.sync.dma_start(w2[:].bitcast(I32), w2_words[0].bitcast(I32))
-        load_scales(w2s, lambda q: w2_scales[0, 4 * q : 4 * q + 4, :])
+        load_scales(nc.sync, wbs, lambda q: wb_scales[:, 0, 4 * q : 4 * q + 4, :].rearrange("e b i -> b e i"))
 
         make_identity(nc, ident[:])
+        warm = keep.tile([P, 8], F32, name="warm", align_bytes=64)
         nc.scalar.activation(warm[:, 0:1], ident[:, 0:1], GELU)
+
+        nc.sync.dma_start(wb[1][:].bitcast(I32), wb_words[1, 0].bitcast(I32))
+        nc.sync.dma_start(wa[:].bitcast(I32), wa_words[:, 0].rearrange("e p b -> p e b").bitcast(I32))
+        load_scales(nc.sync, was, lambda q: wa_scales[:, 0, 4 * q : 4 * q + 4, :].rearrange("e b i -> b e i"))
+        nc.sync.dma_start(w2[:].bitcast(I32), w2_words[0].bitcast(I32))
+        load_scales(nc.sync, w2s, lambda q: w2_scales[0, 4 * q : 4 * q + 4, :])
 
         def offsets(lst, lo, hi):
             return lst[:, lo // 16 : hi // 16]
 
-        def gather(name, lst, lo, hi):
-            words = held(name + "w", [P, hi - lo], U32)
+        def gather(name, lst, lo, hi, tag=None):
+            words = keep.tile([P, hi - lo], U32, name=name + "w", tag=tag or name + "w", align_bytes=64)
             scales = held(name + "s", [P, hi - lo], U8)
             nc.vector.tensor_copy(words[:], xw[:].bitcast(U32).indirect(offsets(lst, lo, hi)))
             nc.vector.tensor_copy(scales[:], xs[:].indirect(offsets(lst, lo, hi)))
@@ -88,9 +89,17 @@ def tile_moe_pool_gelu_kernel(
             ]
 
         tokens_c = gather("gc0", list_c, 0, BLOCK) + gather("gc1", list_c, BLOCK, T)
-        tokens_a = gather("ga0", list_a, 0, HALF) + gather("ga1", list_a, HALF, T)
+        tokens_a = gather("ga0", list_a, 0, T - BLOCK, "gc0w") + gather("ga1", list_a, T - BLOCK, T)
 
-        def expert(tokens, w_words, w_scales, gated, dst):
+        groups = [(0, BLOCK), (BLOCK, HALF), (HALF, T)]
+        c_slots = [held("c_slots%d" % lo, [P, PACK, hi - lo], F32) for lo, hi in groups]
+        g_slots = held("g_slots", [P, PACK, T], F32)
+        c_dst = [c_slots[0][:], c_slots[1][:], c_slots[2][:, :, 0:BLOCK], c_slots[2][:, :, BLOCK:]]
+        blocks = [(tokens_c[s], wb[s // 2][:], wbs[:, s // 2, :], False, c_dst[s]) for s in range(4)]
+        for e in range(E1):
+            blocks.append((tokens_a[e], wa[:, e, :], was[:, e, :], True, g_slots[:, :, e * BLOCK : (e + 1) * BLOCK]))
+
+        def multiply(tokens, w_words, w_scales, gated, dst):
             sums = psum.tile([P, H], F32, name="bank")
             nc.tensor.matmul_mx(
                 out=sums[:], lhsT=tokens[0].bitcast(FP8X4), lhsT_scale=tokens[1],
@@ -102,26 +111,25 @@ def tile_moe_pool_gelu_kernel(
                 nc.scalar.activation(rows[:], by_t, GELU)
             else:
                 nc.scalar.copy(rows[:], by_t)
+            return rows
+
+        def turn(rows, dst):
             turned = psum.tile([P, PACK, BLOCK], F32, name="bank")
             for t in range(PACK):
                 nc.tensor.transpose(turned[:, t, :], rows[:, t, :], ident[:])
             nc.scalar.copy(dst, turned[:])
 
-        c_first = held("c_first", [P, PACK, BLOCK], F32)
-        c_rest = held("c_rest", [P, PACK, T - BLOCK], F32)
-        g_slots = held("g_slots", [P, PACK, T], F32)
-        expert(tokens_c[0], wb[0][:], wbs[:, 0, :], False, c_first[:])
-        for s in range(1, 4):
-            expert(tokens_c[s], wb[s // 2][:], wbs[:, s // 2, :], False, c_rest[:, :, (s - 1) * BLOCK : s * BLOCK])
-        for e in range(E1):
-            expert(tokens_a[e], wa[e // 2][:, e % 2, :], was[:, e, :], True, g_slots[:, :, e * BLOCK : (e + 1) * BLOCK])
+        pending = multiply(*blocks[0])
+        for j in range(len(blocks)):
+            ahead = multiply(*blocks[j + 1]) if j + 1 < len(blocks) else None
+            turn(pending, blocks[j][4])
+            pending = ahead
 
         c_tok = [held("c_tok%d" % t, [P, T], F32) for t in range(PACK)]
         g_tok = [held("g_tok%d" % t, [P, WIDE], F32) for t in range(PACK)]
-        for t in range(PACK):
-            nc.vector.tensor_copy(c_tok[t][:].indirect(offsets(list_c, 0, BLOCK)), c_first[:, t, :])
-        for t in range(PACK):
-            nc.vector.tensor_copy(c_tok[t][:].indirect(offsets(list_c, BLOCK, T)), c_rest[:, t, :])
+        for (lo, hi), src in zip(groups, c_slots):
+            for t in range(PACK):
+                nc.vector.tensor_copy(c_tok[t][:].indirect(offsets(list_c, lo, hi)), src[:, t, :])
 
         h_pair = [held("h_pair%d" % u, [P, 2, T], BF16) for u in range(2)]
         h = held("h", [P, T, PACK], BF16)
@@ -148,15 +156,14 @@ def tile_moe_pool_gelu_kernel(
             )
         for u, cols in enumerate(halves):
             for nb in range(N // P):
-                sums = psum.tile([P, HALF], F32, name="bank")
+                sums = psum_out.tile([P, HALF], F32, name="sums_out")
                 nc.tensor.matmul_mx(
                     out=sums[:], lhsT=w2[:, 2 * P * nb : 2 * P * (nb + 1)].bitcast(FP4X4), lhsT_scale=w2s[:, P * nb : P * (nb + 1)],
                     rhs=codes[u][:].bitcast(FP8X4), rhs_scale=planes[u][:], start=True, stop=True,
                 )
                 result = held("result%d%d" % (u, nb), [P, HALF], F32)
-                if nb == 0:
-                    nc.scalar.copy(result[:], sums[:])
-                    nc.scalar.dma_start(out[P * nb : P * (nb + 1), cols], result[:])
-                else:
+                if (u, nb) == (1, 1):
                     nc.vector.tensor_copy(result[:], sums[:])
-                    nc.sync.dma_start(out[P * nb : P * (nb + 1), cols], result[:])
+                else:
+                    nc.scalar.copy(result[:], sums[:])
+                nc.sync.dma_start(out[P * nb : P * (nb + 1), cols], result[:])

@@ -134,18 +134,18 @@ def tile_moe_pool_gelu_kernel(
         h_pair = [held("h_pair%d" % u, [P, 2, T], BF16) for u in range(2)]
         h = held("h", [P, T, PACK], BF16)
 
-        def product(t, lo, hi):
-            nc.vector.tensor_tensor(h_pair[t // 2][:, t % 2, lo:hi], g_tok[t][:, lo:hi], c_tok[t][:, lo:hi], MULT)
+        def product(engine, t, lo, hi):
+            engine.tensor_tensor(h_pair[t // 2][:, t % 2, lo:hi], g_tok[t][:, lo:hi], c_tok[t][:, lo:hi], MULT)
 
         for t in range(PACK):
             nc.vector.tensor_copy(g_tok[t][:].indirect(list_a[:]), g_slots[:, t, :])
-            if t > 0:
-                product(t - 1, 0, T)
-            if t == 2:
+            if t < PACK - 1:
+                product(nc.gpsimd, t, 0, T)
+            if t == 1:
                 nc.scalar.copy(h[:, :, 0:2], h_pair[0][:].rearrange("p u x -> p x u"))
         halves = [slice(0, HALF), slice(HALF, T)]
         for cols in halves:
-            product(PACK - 1, cols.start, cols.stop)
+            product(nc.vector, PACK - 1, cols.start, cols.stop)
         for cols in halves:
             nc.vector.tensor_copy(h[:, cols, 2:4], h_pair[1][:, :, cols].rearrange("p u x -> p x u"))
         codes = [held("codes%d" % u, [P, HALF], U32) for u in range(2)]

@@ -63,8 +63,8 @@ def tile_moe_pool_gelu_kernel(
         nc.sync.dma_start(list_c[:], offs2)
         load_scales(nc.sync, xs, lambda q: x_scales[0, 4 * q : 4 * q + 4, :])
         nc.scalar.dma_start(wb[0][:].bitcast(I32), wb_words[0, 0].bitcast(I32))
-        nc.sync.dma_start(list_a[:], offs)
         load_scales(nc.sync, wbs, lambda q: wb_scales[:, 0, 4 * q : 4 * q + 4, :].rearrange("e b i -> b e i"))
+        nc.sync.dma_start(list_a[:], offs)
 
         make_identity(nc, ident[:])
         warm = keep.tile([P, 8], F32, name="warm", align_bytes=64)
@@ -89,47 +89,58 @@ def tile_moe_pool_gelu_kernel(
             ]
 
         tokens_c = gather("gc0", list_c, 0, BLOCK) + gather("gc1", list_c, BLOCK, T)
-        tokens_a = gather("ga0", list_a, 0, T - BLOCK, "gc0w") + gather("ga1", list_a, T - BLOCK, T)
+        tokens_a = gather("ga0", list_a, 0, HALF) + gather("ga1", list_a, HALF, T)
 
-        groups = [(0, BLOCK), (BLOCK, HALF), (HALF, T)]
-        c_slots = [held("c_slots%d" % lo, [P, PACK, hi - lo], F32) for lo, hi in groups]
-        g_slots = held("g_slots", [P, PACK, T], F32)
-        c_dst = [c_slots[0][:], c_slots[1][:], c_slots[2][:, :, 0:BLOCK], c_slots[2][:, :, BLOCK:]]
-        blocks = [(tokens_c[s], wb[s // 2][:], wbs[:, s // 2, :], False, c_dst[s]) for s in range(4)]
-        for e in range(E1):
-            blocks.append((tokens_a[e], wa[:, e, :], was[:, e, :], True, g_slots[:, :, e * BLOCK : (e + 1) * BLOCK]))
-
-        def multiply(tokens, w_words, w_scales, gated, dst):
-            sums = psum.tile([P, H], F32, name="bank")
+        def multiply(tokens, w_words, w_scales):
+            sums = psum.tile([P, H], F32, name="sums")
             nc.tensor.matmul_mx(
                 out=sums[:], lhsT=tokens[0].bitcast(FP8X4), lhsT_scale=tokens[1],
                 rhs=w_words.bitcast(FP4X4), rhs_scale=w_scales, start=True, stop=True,
             )
-            rows = stage.tile([P, PACK, P], F32, name="rows")
-            by_t = sums[:].rearrange("s (p t) -> s t p", t=PACK)
+            return sums[:].rearrange("s (p t) -> s t p", t=PACK)
+
+        def leave(by_t, gated, name):
+            rows = stage.tile(list(by_t.shape), F32, name=name)
             if gated:
                 nc.scalar.activation(rows[:], by_t, GELU)
             else:
                 nc.scalar.copy(rows[:], by_t)
             return rows
 
-        def turn(rows, dst):
-            turned = psum.tile([P, PACK, BLOCK], F32, name="bank")
-            for t in range(PACK):
+        def turn(rows, turned, dst):
+            for t in range(rows.shape[1]):
                 nc.tensor.transpose(turned[:, t, :], rows[:, t, :], ident[:])
             nc.scalar.copy(dst, turned[:])
 
-        pending = multiply(*blocks[0])
+        c_head = [held("c_head%d" % u, [P, 2, BLOCK], F32) for u in range(2)]
+        c_slots = {s: held("c_slots%d" % s, [P, PACK, BLOCK], F32) for s in range(1, 4)}
+        g_slots = held("g_slots", [P, PACK, T], F32)
+
+        first = multiply(tokens_c[0], wb[0][:], wbs[:, 0, :])
+        head_rows = [leave(first[:, 2 * u : 2 * u + 2, :], False, "head_rows") for u in range(2)]
+        for u in range(2):
+            turn(head_rows[u], psum_out.tile([P, 2, BLOCK], F32, name="sums_out"), c_head[u][:])
+
+        blocks = [(tokens_c[s], wb[s // 2][:], wbs[:, s // 2, :], False, c_slots[s][:]) for s in range(1, 4)]
+        for e in range(E1):
+            blocks.append((tokens_a[e], wa[:, e, :], was[:, e, :], True, g_slots[:, :, e * BLOCK : (e + 1) * BLOCK]))
+
+        def rows_of(block):
+            return leave(multiply(*block[:3]), block[3], "rows")
+
+        pending = rows_of(blocks[0])
         for j in range(len(blocks)):
-            ahead = multiply(*blocks[j + 1]) if j + 1 < len(blocks) else None
-            turn(pending, blocks[j][4])
+            ahead = rows_of(blocks[j + 1]) if j + 1 < len(blocks) else None
+            turn(pending, psum.tile([P, PACK, BLOCK], F32, name="turned"), blocks[j][4])
             pending = ahead
 
         c_tok = [held("c_tok%d" % t, [P, T], F32) for t in range(PACK)]
         g_tok = [held("g_tok%d" % t, [P, WIDE], F32) for t in range(PACK)]
-        for (lo, hi), src in zip(groups, c_slots):
+        for t in range(PACK):
+            nc.vector.tensor_copy(c_tok[t][:].indirect(offsets(list_c, 0, BLOCK)), c_head[t // 2][:, t % 2, :])
+        for s in range(1, 4):
             for t in range(PACK):
-                nc.vector.tensor_copy(c_tok[t][:].indirect(offsets(list_c, lo, hi)), src[:, t, :])
+                nc.vector.tensor_copy(c_tok[t][:].indirect(offsets(list_c, s * BLOCK, (s + 1) * BLOCK)), c_slots[s][:, t, :])
 
         h_pair = [held("h_pair%d" % u, [P, 2, T], BF16) for u in range(2)]
         h = held("h", [P, T, PACK], BF16)
@@ -166,4 +177,5 @@ def tile_moe_pool_gelu_kernel(
                     nc.vector.tensor_copy(result[:], sums[:])
                 else:
                     nc.scalar.copy(result[:], sums[:])
-                nc.sync.dma_start(out[P * nb : P * (nb + 1), cols], result[:])
+                queue = nc.scalar if (u, nb) == (1, 0) else nc.sync
+                queue.dma_start(out[P * nb : P * (nb + 1), cols], result[:])

from contextlib import ExitStack

import concourse.mybir as mybir
from concourse.masks import make_identity

K, T, H, N = 512, 512, 512, 256
E1, E2 = 4, 2
FLOPS = 2 * K * H * T * 2 + 2 * H * N * T

F32 = mybir.dt.float32
BF16 = mybir.dt.bfloat16
I32 = mybir.dt.int32
U32 = mybir.dt.uint32
U16 = mybir.dt.uint16
U8 = mybir.dt.uint8
FP8X4 = mybir.dt.float8_e4m3fn_x4
FP4X4 = mybir.dt.float4_e2m1fn_x4
GELU = mybir.ActivationFunctionType.Gelu_apprx_tanh
MULT = mybir.AluOpType.mult

P = 128
PACK = 4
BLOCK = 128
WIDE = 704
HALF = T // 2


def tile_moe_pool_gelu_kernel(
    tc, x_words, x_scales, wa_words, wa_scales, wb_words, wb_scales, w2_words, w2_scales, offs, offs2, out
):
    nc = tc.nc
    with ExitStack() as ctx:
        keep = ctx.enter_context(tc.tile_pool(name="keep", bufs=1))
        stage = ctx.enter_context(tc.tile_pool(name="stage", bufs=2))
        psum = ctx.enter_context(tc.psum_pool(name="psum", bufs=2))
        psum_out = ctx.enter_context(tc.psum_pool(name="psum_out", bufs=4))

        def held(name, shape, dtype):
            return keep.tile(shape, dtype, name=name, align_bytes=64)

        list_a = held("list_a", [P, T // 16], U16)
        list_c = held("list_c", [P, T // 16], U16)
        xw = held("xw", [P, T], I32)
        xs = held("xs", [P, T], U8)
        wb = [held("wb%d" % f, [P, 2 * H], U8) for f in range(E2)]
        wa = held("wa", [P, E1, 2 * H], U8)
        w2 = held("w2", [P, 2 * N], U8)
        was = held("was", [P, E1, H], U8)
        wbs = held("wbs", [P, E2, H], U8)
        w2s = held("w2s", [P, N], U8)
        ident = held("ident", [P, P], F32)

        nc.gpsimd.memset(xs[:].bitcast(I32), 0)
        nc.gpsimd.memset(wbs[:].bitcast(I32), 0)
        nc.vector.memset(was[:].bitcast(I32), 0)
        nc.vector.memset(w2s[:].bitcast(I32), 0)

        def load_scales(queue, plane, rows):
            for q in range(4):
                queue.dma_start(plane[32 * q : 32 * q + 4].bitcast(I32), rows(q).bitcast(I32))

        nc.scalar.dma_start(xw[:], x_words[0].rearrange("p t d -> p (t d)").bitcast(I32))
        nc.sync.dma_start(list_c[:], offs2)
        load_scales(nc.sync, xs, lambda q: x_scales[0, 4 * q : 4 * q + 4, :])
        nc.scalar.dma_start(wb[0][:].bitcast(I32), wb_words[0, 0].bitcast(I32))
        load_scales(nc.sync, wbs, lambda q: wb_scales[:, 0, 4 * q : 4 * q + 4, :].rearrange("e b i -> b e i"))
        nc.sync.dma_start(list_a[:], offs)

        make_identity(nc, ident[:])
        warm = keep.tile([P, 8], F32, name="warm", align_bytes=64)
        nc.scalar.activation(warm[:, 0:1], ident[:, 0:1], GELU)

        nc.sync.dma_start(wb[1][:].bitcast(I32), wb_words[1, 0].bitcast(I32))
        nc.sync.dma_start(wa[:].bitcast(I32), wa_words[:, 0].rearrange("e p b -> p e b").bitcast(I32))
        load_scales(nc.sync, was, lambda q: wa_scales[:, 0, 4 * q : 4 * q + 4, :].rearrange("e b i -> b e i"))
        nc.sync.dma_start(w2[:].bitcast(I32), w2_words[0].bitcast(I32))
        load_scales(nc.sync, w2s, lambda q: w2_scales[0, 4 * q : 4 * q + 4, :])

        def offsets(lst, lo, hi):
            return lst[:, lo // 16 : hi // 16]

        def gather(name, lst, lo, hi, tag=None):
            words = keep.tile([P, hi - lo], U32, name=name + "w", tag=tag or name + "w", align_bytes=64)
            scales = held(name + "s", [P, hi - lo], U8)
            nc.vector.tensor_copy(words[:], xw[:].bitcast(U32).indirect(offsets(lst, lo, hi)))
            nc.vector.tensor_copy(scales[:], xs[:].indirect(offsets(lst, lo, hi)))
            return [
                (words[:, j : j + BLOCK], scales[:, j : j + BLOCK]) for j in range(0, hi - lo, BLOCK)
            ]

        tokens_c = gather("gc0", list_c, 0, BLOCK) + gather("gc1", list_c, BLOCK, T)
        tokens_a = gather("ga0", list_a, 0, HALF) + gather("ga1", list_a, HALF, T)

        def multiply(tokens, w_words, w_scales):
            sums = psum.tile([P, H], F32, name="sums")
            nc.tensor.matmul_mx(
                out=sums[:], lhsT=tokens[0].bitcast(FP8X4), lhsT_scale=tokens[1],
                rhs=w_words.bitcast(FP4X4), rhs_scale=w_scales, start=True, stop=True,
            )
            return sums[:].rearrange("s (p t) -> s t p", t=PACK)

        def leave(by_t, gated, name):
            rows = stage.tile(list(by_t.shape), F32, name=name)
            if gated:
                nc.scalar.activation(rows[:], by_t, GELU)
            else:
                nc.scalar.copy(rows[:], by_t)
            return rows

        def turn(rows, turned, dst):
            for t in range(rows.shape[1]):
                nc.tensor.transpose(turned[:, t, :], rows[:, t, :], ident[:])
            nc.scalar.copy(dst, turned[:])

        c_head = [held("c_head%d" % u, [P, 2, BLOCK], F32) for u in range(2)]
        c_slots = {s: held("c_slots%d" % s, [P, PACK, BLOCK], F32) for s in range(1, 4)}
        g_slots = held("g_slots", [P, PACK, T], F32)

        first = multiply(tokens_c[0], wb[0][:], wbs[:, 0, :])
        head_rows = [leave(first[:, 2 * u : 2 * u + 2, :], False, "head_rows") for u in range(2)]
        for u in range(2):
            turn(head_rows[u], psum_out.tile([P, 2, BLOCK], F32, name="sums_out"), c_head[u][:])

        blocks = [(tokens_c[s], wb[s // 2][:], wbs[:, s // 2, :], False, c_slots[s][:]) for s in range(1, 4)]
        for e in range(E1):
            blocks.append((tokens_a[e], wa[:, e, :], was[:, e, :], True, g_slots[:, :, e * BLOCK : (e + 1) * BLOCK]))

        def rows_of(block):
            return leave(multiply(*block[:3]), block[3], "rows")

        pending = rows_of(blocks[0])
        for j in range(len(blocks)):
            ahead = rows_of(blocks[j + 1]) if j + 1 < len(blocks) else None
            turn(pending, psum.tile([P, PACK, BLOCK], F32, name="turned"), blocks[j][4])
            pending = ahead

        c_tok = [held("c_tok%d" % t, [P, T], F32) for t in range(PACK)]
        g_tok = [held("g_tok%d" % t, [P, WIDE], F32) for t in range(PACK)]
        for t in range(PACK):
            nc.vector.tensor_copy(c_tok[t][:].indirect(offsets(list_c, 0, BLOCK)), c_head[t // 2][:, t % 2, :])
        for s in range(1, 4):
            for t in range(PACK):
                nc.vector.tensor_copy(c_tok[t][:].indirect(offsets(list_c, s * BLOCK, (s + 1) * BLOCK)), c_slots[s][:, t, :])

        h_pair = [held("h_pair%d" % u, [P, 2, T], BF16) for u in range(2)]
        h = held("h", [P, T, PACK], BF16)

        def product(engine, t, lo, hi):
            engine.tensor_tensor(h_pair[t // 2][:, t % 2, lo:hi], g_tok[t][:, lo:hi], c_tok[t][:, lo:hi], MULT)

        for t in range(PACK):
            nc.vector.tensor_copy(g_tok[t][:].indirect(list_a[:]), g_slots[:, t, :])
            if t < PACK - 1:
                product(nc.gpsimd, t, 0, T)
            if t == 1:
                nc.scalar.copy(h[:, :, 0:2], h_pair[0][:].rearrange("p u x -> p x u"))
        halves = [slice(0, HALF), slice(HALF, T)]
        for cols in halves:
            product(nc.vector, PACK - 1, cols.start, cols.stop)
        for cols in halves:
            nc.vector.tensor_copy(h[:, cols, 2:4], h_pair[1][:, :, cols].rearrange("p u x -> p x u"))
        codes = [held("codes%d" % u, [P, HALF], U32) for u in range(2)]
        planes = [held("planes%d" % u, [P, HALF], U8) for u in range(2)]
        for u, cols in enumerate(halves):
            nc.vector.quantize_mx(
                out=codes[u][:].bitcast(FP8X4), scales=planes[u][:], in_=h[:, cols, :].rearrange("p x t -> p (x t)")
            )
        for u, cols in enumerate(halves):
            for nb in range(N // P):
                sums = psum_out.tile([P, HALF], F32, name="sums_out")
                nc.tensor.matmul_mx(
                    out=sums[:], lhsT=w2[:, 2 * P * nb : 2 * P * (nb + 1)].bitcast(FP4X4), lhsT_scale=w2s[:, P * nb : P * (nb + 1)],
                    rhs=codes[u][:].bitcast(FP8X4), rhs_scale=planes[u][:], start=True, stop=True,
                )
                result = held("result%d%d" % (u, nb), [P, HALF], F32)
                if (u, nb) == (1, 1):
                    nc.vector.tensor_copy(result[:], sums[:])
                else:
                    nc.scalar.copy(result[:], sums[:])
                queue = nc.scalar if (u, nb) == (1, 0) else nc.sync
                queue.dma_start(out[P * nb : P * (nb + 1), cols], result[:])
